import numpy as np
import ml_dtypes


def mxq(x, axis, fmt="e4m3"):
    dtype, down = {"e4m3": (ml_dtypes.float8_e4m3fn, 7), "e5m2": (ml_dtypes.float8_e5m2, 14)}[fmt]
    v = np.moveaxis(np.asarray(x, np.float32).astype(ml_dtypes.bfloat16).astype(np.float64), axis, -1)
    blocks = v.reshape(v.shape[:-1] + (-1, 32))
    amax = np.abs(blocks).max(-1, keepdims=True)
    byte = np.maximum(np.where(amax > 0, np.frexp(amax)[1] - 1 + 127, 0) - down, 1)
    scale = np.exp2(byte - 127.0)
    codes = (blocks / scale).astype(np.float32).astype(dtype).astype(np.float64)
    return np.moveaxis((codes * scale).reshape(v.shape), -1, axis)


WIDE = False


def mx_kscale(k):
    if not WIDE:
        return np.ones(k)
    levels = np.array([10, -10, 5, -5, 0])
    if k % 512:
        return np.exp2(np.random.permutation(np.resize(levels, k // 32))).repeat(32)
    a = np.empty((k // 512, 16))
    for p in range(k // 512):
        a[p, :8] = np.random.permutation(np.resize(levels, 8))
        for g in range(8):
            far = levels[np.abs(levels - a[p, g]) >= 10]
            a[p, g + 8] = far[np.random.randint(len(far))]
    return np.exp2(a.ravel()).repeat(32)


def f64(x):
    return np.asarray(x).astype(np.float64)


def striped(idx):
    return np.tile(idx.reshape(-1, 16).T, (8, 1)).astype(np.uint16)


def unstriped(offs):
    return offs[:16].T.reshape(-1).astype(np.int64)


def pack_weight(w):
    k, n = w.shape
    w = f64(np.asarray(w, np.float32).astype(ml_dtypes.bfloat16)).reshape(k // 32, 32, n)
    amax = np.abs(w).max(1)
    byte = np.clip(np.where(amax > 0, np.frexp(amax)[1] - 1 + 127 - 7, 1), 1, 254)
    scaled = (w * np.exp2(127.0 - byte)[:, None, :]).reshape(k, n).astype(np.float32)
    words = np.ascontiguousarray(scaled.reshape(k // 512, 128, 4, n).transpose(0, 1, 3, 2)).astype(ml_dtypes.float8_e4m3fn).view(np.uint8)
    return words, np.ascontiguousarray(byte.astype(np.uint8).reshape(k // 512, 16, n))


def unpack_weight(words, scales):
    g, p, n, _ = words.shape
    vals = np.ascontiguousarray(words).view(ml_dtypes.float8_e4m3fn).astype(np.float64) * np.repeat(np.exp2(scales.astype(np.float64) - 127.0), 8, axis=1)[..., None]
    return vals.transpose(0, 1, 3, 2).reshape(g * 512, n)


K, T, S, H, D, W, U = 512, 1024, 512, 512, 4, 2048, 512


def setup_inputs():
    n = np.random.standard_normal
    s = mx_kscale(K)[:, None]
    u = mx_kscale(H)
    packed_xT = pack_weight(n((K, T)) * s)
    packed_eT = pack_weight(n((H, W)) / np.sqrt(H) / u[:, None])
    return {
        "x_words": packed_xT[0],
        "x_scales": packed_xT[1],
        "w1": (n((K, H)) / np.sqrt(K) / s * u).astype(np.float32),
        "e_words": packed_eT[0],
        "e_scales": packed_eT[1],
        "offs": striped(np.random.permutation(T)[:S]),
        "pos": striped(np.random.permutation(W)[:U]),
        "neg": striped(np.random.permutation(W)[:U]),
    }


def reference(x_words, x_scales, w1, e_words, e_scales, offs, pos, neg):
    xq = unpack_weight(x_words, x_scales)[:, unstriped(offs)]
    h = mxq(f64(w1), 0, "e4m3").T @ xq
    hq = mxq(h, 0, "e4m3")
    e_neg = unpack_weight(e_words, e_scales)[:, unstriped(neg)]
    z = hq.T @ e_neg
    neg1 = z.reshape(len(z), -1, D).max(axis=2)
    e_pos = unpack_weight(e_words, e_scales)[:, unstriped(pos)]
    y = hq.T @ e_pos
    pos1 = y.reshape(len(y), -1, D).min(axis=2)
    return np.log(np.exp(neg1 - pos1 + 0.3) + 1.0)

@@ -1,0 +1,141 @@
+from contextlib import ExitStack
+
+import concourse.mybir as mybir
+
+F32 = mybir.dt.float32
+BF16 = mybir.dt.bfloat16
+I32 = mybir.dt.int32
+U32 = mybir.dt.uint32
+U16 = mybir.dt.uint16
+U8 = mybir.dt.uint8
+FP8X4 = mybir.dt.float8_e4m3fn_x4
+ALU = mybir.AluOpType
+ACT = mybir.ActivationFunctionType
+AXIS = mybir.AxisListType
+
+P = 128
+PACK = 4
+K, T, S, H, D, W, U = 512, 1024, 512, 512, 4, 2048, 512
+V = U // D
+BLOCKS = S // P
+MARGIN = 0.3
+EXP_CAP = 2.0 ** 60
+
+FLOPS = 2 * K * H * S + 2 * 2 * H * S * U
+
+
+def tile_picked_yhard_soft_p_kernel(
+    tc, x_words, x_scales, w1, e_words, e_scales, offs, pos, neg, out
+):
+    nc = tc.nc
+    with ExitStack() as ctx:
+        keep = ctx.enter_context(tc.tile_pool(name="keep", bufs=1))
+        psum = ctx.enter_context(tc.psum_pool(name="psum", bufs=4))
+
+        offs_t = keep.tile([P, S // 16], U16, name="offs_t")
+        neg_t = keep.tile([P, U // 16], U16, name="neg_t")
+        pos_t = keep.tile([P, U // 16], U16, name="pos_t")
+        xs = keep.tile([P, T], U8, name="xs", align_bytes=64)
+        es = keep.tile([P, W], U8, name="es", align_bytes=64)
+        xw = keep.tile([P, T], I32, name="xw", align_bytes=64)
+        ew = keep.tile([P, W], I32, name="ew", align_bytes=64)
+        w_raw = [keep.tile([P, PACK, H // 2], F32, name=f"w_raw{h}") for h in range(2)]
+        warm = keep.tile([P, 1], F32, name="warm")
+        warm2 = keep.tile([P, 1], F32, name="warm2")
+
+        nc.vector.memset(xs[:].bitcast(I32), 0)
+        nc.vector.memset(es[:].bitcast(I32), 0)
+        nc.vector.memset(warm[:], 0.0)
+        nc.scalar.activation(warm2[:], warm[:], ACT.Exp)
+
+        def load_scales(tile, scales):
+            for q in range(4):
+                nc.sync.dma_start(tile[32 * q : 32 * q + 4, :].bitcast(I32), scales[0, 4 * q : 4 * q + 4, :].bitcast(I32))
+
+        w_rows = w1.rearrange("(p j) c -> p j c", j=PACK)
+        nc.sync.dma_start(offs_t[:], offs)
+        nc.sync.dma_start(neg_t[:], neg)
+        nc.sync.dma_start(pos_t[:], pos)
+        nc.sync.dma_start(xw[:], x_words[0].rearrange("p n t -> p (n t)").bitcast(I32))
+        load_scales(xs, x_scales)
+        nc.sync.dma_start(w_raw[0][:], w_rows[:, :, : H // 2])
+        load_scales(es, e_scales)
+        nc.sync.dma_start(w_raw[1][:], w_rows[:, :, H // 2 :])
+        nc.sync.dma_start(ew[:], e_words[0].rearrange("p n t -> p (n t)").bitcast(I32))
+
+        xs_g = keep.tile([P, S], U8, name="xs_g", align_bytes=64)
+        xw_g = keep.tile([P, S], U32, name="xw_g", align_bytes=64)
+        ns_g = keep.tile([P, U], U8, name="ns_g", align_bytes=64)
+        nw_g = keep.tile([P, U], U32, name="nw_g", align_bytes=64)
+        ps_g = keep.tile([P, U], U8, name="ps_g", align_bytes=64)
+        pw_g = keep.tile([P, U], U32, name="pw_g", align_bytes=64)
+
+        nc.vector.tensor_copy(xw_g[:], xw[:].bitcast(U32).indirect(offs_t[:]))
+        nc.vector.tensor_copy(xs_g[:], xs[:].indirect(offs_t[:]))
+        nc.vector.tensor_copy(ns_g[:], es[:].indirect(neg_t[:]))
+        nc.vector.tensor_copy(ps_g[:], es[:].indirect(pos_t[:]))
+
+        w_bf = keep.tile([P, PACK * H], BF16, name="w_bf", align_bytes=64)
+        w_view = w_bf[:].rearrange("p (t m j) -> p m t j", t=PACK, j=PACK)
+        for h in range(2):
+            nc.scalar.copy(
+                w_view[:, h * (P // 2) : (h + 1) * (P // 2), :, :],
+                w_raw[h][:].rearrange("p j (m t) -> p m t j", t=PACK),
+            )
+        w_q = keep.tile([P, H], U32, name="w_q", align_bytes=64)
+        w_s = keep.tile([P, H], U8, name="w_s", align_bytes=64)
+        nc.vector.quantize_mx(out=w_q[:].bitcast(FP8X4), scales=w_s[:], in_=w_bf[:])
+
+        h_q, h_s = [], []
+        h_bf = []
+        for b in range(BLOCKS):
+            cols = slice(b * P, (b + 1) * P)
+            bank = psum.tile([P, PACK, P], F32, name="hy", tag="hy")
+            for t in range(PACK):
+                wc = slice(t * P, (t + 1) * P)
+                nc.tensor.matmul_mx(
+                    out=bank[:, t, :], lhsT=w_q[:, wc].bitcast(FP8X4), lhsT_scale=w_s[:, wc],
+                    rhs=xw_g[:, cols].bitcast(FP8X4), rhs_scale=xs_g[:, cols], start=True, stop=True,
+                )
+            hb = keep.tile([P, P * PACK], BF16, name=f"h_bf{b}", align_bytes=64)
+            nc.scalar.copy(hb[:].rearrange("p (n t) -> p n t", t=PACK), bank[:].rearrange("p t n -> p n t"))
+            h_bf.append(hb)
+
+        nc.vector.tensor_copy(nw_g[:], ew[:].bitcast(U32).indirect(neg_t[:]))
+        for b in range(BLOCKS):
+            hq = keep.tile([P, P], U32, name=f"h_q{b}", align_bytes=64)
+            hs = keep.tile([P, P], U8, name=f"h_s{b}", align_bytes=64)
+            nc.vector.quantize_mx(out=hq[:].bitcast(FP8X4), scales=hs[:], in_=h_bf[b][:])
+            h_q.append(hq)
+            h_s.append(hs)
+        nc.vector.tensor_copy(pw_g[:], ew[:].bitcast(U32).indirect(pos_t[:]))
+
+        neg1 = [keep.tile([P, V], F32, name=f"neg1_{b}") for b in range(BLOCKS)]
+        pos1 = [keep.tile([P, V], F32, name=f"pos1_{b}") for b in range(BLOCKS)]
+        for b in range(BLOCKS):
+            z = psum.tile([P, V, D], F32, name="z", tag="z")
+            nc.tensor.matmul_mx(
+                out=z[:].rearrange("p v d -> p (v d)"), lhsT=h_q[b][:].bitcast(FP8X4), lhsT_scale=h_s[b][:],
+                rhs=nw_g[:].bitcast(FP8X4), rhs_scale=ns_g[:], start=True, stop=True,
+            )
+            nc.vector.tensor_reduce(neg1[b][:], z[:], AXIS.X, ALU.max)
+        u = [keep.tile([P, V], F32, name=f"u{b}") for b in range(BLOCKS)]
+        e = keep.tile([P, BLOCKS, V], F32, name="e")
+        for b in range(BLOCKS):
+            y = psum.tile([P, PACK, P], F32, name="hy", tag="hy")
+            flat = y[:].rearrange("p a n -> p (a n)")
+            nc.tensor.matmul_mx(
+                out=flat, lhsT=h_q[b][:].bitcast(FP8X4), lhsT_scale=h_s[b][:],
+                rhs=pw_g[:].bitcast(FP8X4), rhs_scale=ps_g[:], start=True, stop=True,
+            )
+            nc.vector.tensor_reduce(pos1[b][:], flat.rearrange("p (v d) -> p v d", d=D), AXIS.X, ALU.min)
+            nc.vector.scalar_tensor_tensor(u[b][:], neg1[b][:], MARGIN, pos1[b][:], ALU.add, ALU.subtract)
+            nc.scalar.activation(e[:, b, :], u[b][:], ACT.Exp)
+        ec = keep.tile([P, BLOCKS, V], F32, name="ec")
+        nc.vector.tensor_scalar(ec[:], e[:], EXP_CAP, None, ALU.min)
+        for b in range(BLOCKS):
+            lg = keep.tile([P, V], F32, name=f"lg{b}")
+            res = keep.tile([P, V], F32, name=f"res{b}")
+            nc.scalar.activation(lg[:], ec[:, b, :], ACT.Ln, bias=1.0)
+            nc.vector.tensor_tensor(res[:], u[b][:], lg[:], ALU.max)
+            nc.sync.dma_start(out[b * P : (b + 1) * P, :], res[:])

@@ -38,15 +38,12 @@ def tile_picked_yhard_soft_p_kernel(
         xs = keep.tile([P, T], U8, name="xs", align_bytes=64)
         es = keep.tile([P, W], U8, name="es", align_bytes=64)
         xw = keep.tile([P, T], I32, name="xw", align_bytes=64)
-        ew = keep.tile([P, W], I32, name="ew", align_bytes=64)
+        ew = keep.tile([P, W], I32, name="ew", tag="e_words_then_h_codes", align_bytes=64)
         w_raw = [keep.tile([P, PACK, H // 2], F32, name=f"w_raw{h}") for h in range(2)]
-        warm = keep.tile([P, 1], F32, name="warm")
-        warm2 = keep.tile([P, 1], F32, name="warm2")
 
+        nc.vector.memset(es[:, : W // 2].bitcast(I32), 0)
+        nc.gpsimd.memset(es[:, W // 2 :].bitcast(I32), 0)
         nc.vector.memset(xs[:].bitcast(I32), 0)
-        nc.vector.memset(es[:].bitcast(I32), 0)
-        nc.vector.memset(warm[:], 0.0)
-        nc.scalar.activation(warm2[:], warm[:], ACT.Exp)
 
         def load_scales(tile, scales):
             for q in range(4):
@@ -54,13 +51,13 @@ def tile_picked_yhard_soft_p_kernel(
 
         w_rows = w1.rearrange("(p j) c -> p j c", j=PACK)
         nc.sync.dma_start(offs_t[:], offs)
+        nc.sync.dma_start(xw[:], x_words[0].rearrange("p n t -> p (n t)").bitcast(I32))
         nc.sync.dma_start(neg_t[:], neg)
         nc.sync.dma_start(pos_t[:], pos)
-        nc.sync.dma_start(xw[:], x_words[0].rearrange("p n t -> p (n t)").bitcast(I32))
-        load_scales(xs, x_scales)
-        nc.sync.dma_start(w_raw[0][:], w_rows[:, :, : H // 2])
         load_scales(es, e_scales)
-        nc.sync.dma_start(w_raw[1][:], w_rows[:, :, H // 2 :])
+        for h in range(2):
+            nc.sync.dma_start(w_raw[h][:], w_rows[:, :, h * (H // 2) : (h + 1) * (H // 2)])
+        load_scales(xs, x_scales)
         nc.sync.dma_start(ew[:], e_words[0].rearrange("p n t -> p (n t)").bitcast(I32))
 
         xs_g = keep.tile([P, S], U8, name="xs_g", align_bytes=64)
@@ -71,16 +68,16 @@ def tile_picked_yhard_soft_p_kernel(
         pw_g = keep.tile([P, U], U32, name="pw_g", align_bytes=64)
 
         nc.vector.tensor_copy(xw_g[:], xw[:].bitcast(U32).indirect(offs_t[:]))
-        nc.vector.tensor_copy(xs_g[:], xs[:].indirect(offs_t[:]))
         nc.vector.tensor_copy(ns_g[:], es[:].indirect(neg_t[:]))
         nc.vector.tensor_copy(ps_g[:], es[:].indirect(pos_t[:]))
+        nc.vector.tensor_copy(xs_g[:], xs[:].indirect(offs_t[:]))
 
         w_bf = keep.tile([P, PACK * H], BF16, name="w_bf", align_bytes=64)
         w_view = w_bf[:].rearrange("p (t m j) -> p m t j", t=PACK, j=PACK)
         for h in range(2):
-            nc.scalar.copy(
+            nc.scalar.activation(
                 w_view[:, h * (P // 2) : (h + 1) * (P // 2), :, :],
-                w_raw[h][:].rearrange("p j (m t) -> p m t j", t=PACK),
+                w_raw[h][:].rearrange("p j (m t) -> p m t j", t=PACK), ACT.Copy,
             )
         w_q = keep.tile([P, H], U32, name="w_q", align_bytes=64)
         w_s = keep.tile([P, H], U8, name="w_s", align_bytes=64)
@@ -102,40 +99,62 @@ def tile_picked_yhard_soft_p_kernel(
             h_bf.append(hb)
 
         nc.vector.tensor_copy(nw_g[:], ew[:].bitcast(U32).indirect(neg_t[:]))
+        nc.vector.tensor_copy(pw_g[:], ew[:].bitcast(U32).indirect(pos_t[:]))
+        h_codes = keep.tile([P, S], U32, name="h_codes", tag="e_words_then_h_codes", align_bytes=64)
         for b in range(BLOCKS):
-            hq = keep.tile([P, P], U32, name=f"h_q{b}", align_bytes=64)
+            hq = h_codes[:, b * P : (b + 1) * P]
             hs = keep.tile([P, P], U8, name=f"h_s{b}", align_bytes=64)
-            nc.vector.quantize_mx(out=hq[:].bitcast(FP8X4), scales=hs[:], in_=h_bf[b][:])
+            nc.vector.quantize_mx(out=hq.bitcast(FP8X4), scales=hs[:], in_=h_bf[b][:])
             h_q.append(hq)
             h_s.append(hs)
-        nc.vector.tensor_copy(pw_g[:], ew[:].bitcast(U32).indirect(pos_t[:]))
 
-        neg1 = [keep.tile([P, V], F32, name=f"neg1_{b}") for b in range(BLOCKS)]
-        pos1 = [keep.tile([P, V], F32, name=f"pos1_{b}") for b in range(BLOCKS)]
-        for b in range(BLOCKS):
-            z = psum.tile([P, V, D], F32, name="z", tag="z")
-            nc.tensor.matmul_mx(
-                out=z[:].rearrange("p v d -> p (v d)"), lhsT=h_q[b][:].bitcast(FP8X4), lhsT_scale=h_s[b][:],
-                rhs=nw_g[:].bitcast(FP8X4), rhs_scale=ns_g[:], start=True, stop=True,
-            )
-            nc.vector.tensor_reduce(neg1[b][:], z[:], AXIS.X, ALU.max)
-        u = [keep.tile([P, V], F32, name=f"u{b}") for b in range(BLOCKS)]
+        u = keep.tile([P, BLOCKS, V], F32, name="u")
         e = keep.tile([P, BLOCKS, V], F32, name="e")
-        for b in range(BLOCKS):
-            y = psum.tile([P, PACK, P], F32, name="hy", tag="hy")
-            flat = y[:].rearrange("p a n -> p (a n)")
-            nc.tensor.matmul_mx(
-                out=flat, lhsT=h_q[b][:].bitcast(FP8X4), lhsT_scale=h_s[b][:],
-                rhs=pw_g[:].bitcast(FP8X4), rhs_scale=ps_g[:], start=True, stop=True,
-            )
-            nc.vector.tensor_reduce(pos1[b][:], flat.rearrange("p (v d) -> p v d", d=D), AXIS.X, ALU.min)
-            nc.vector.scalar_tensor_tensor(u[b][:], neg1[b][:], MARGIN, pos1[b][:], ALU.add, ALU.subtract)
-            nc.scalar.activation(e[:, b, :], u[b][:], ACT.Exp)
+        pairs = [None] + [keep.tile([P, 2, 2, V], F32, name=f"pairs{b}") for b in range(1, BLOCKS)]
+        tops = [keep.tile([P, 2, V], F32, name=f"tops{b}") for b in range(BLOCKS)]
+
+        def scores(b):
+            z = psum.tile([P, U], F32, name="z", tag="z")
+            y = psum.tile([P, U], F32, name="hy", tag="hy")
+            for bank, words, planes in ((z, nw_g, ns_g), (y, pw_g, ps_g)):
+                nc.tensor.matmul_mx(
+                    out=bank[:], lhsT=h_q[b].bitcast(FP8X4), lhsT_scale=h_s[b][:],
+                    rhs=words[:].bitcast(FP8X4), rhs_scale=planes[:], start=True, stop=True,
+                )
+            if b == 0:
+                nc.vector.tensor_reduce(tops[b][:, 0, :], z[:].rearrange("p (v d) -> p v d", d=D), AXIS.X, ALU.max)
+                nc.vector.tensor_reduce(tops[b][:, 1, :], y[:].rearrange("p (v d) -> p v d", d=D), AXIS.X, ALU.min)
+                return
+            z_d = z[:].rearrange("p (v d) -> p d v", d=D)
+            y_d = y[:].rearrange("p (v d) -> p d v", d=D)
+            z_lo = keep.tile([P, 2, V], F32, name=f"z_lo{b}")
+            y_lo = keep.tile([P, 2, V], F32, name=f"y_lo{b}")
+            nc.scalar.copy(z_lo[:], z_d[:, 0:2, :])
+            nc.scalar.activation(y_lo[:], y_d[:, 0:2, :], ACT.Copy, scale=-1.0)
+            nc.vector.tensor_tensor(pairs[b][:, :, 0, :], z_d[:, 2:4, :], z_lo[:], ALU.max)
+            nc.vector.scalar_tensor_tensor(pairs[b][:, :, 1, :], y_d[:, 2:4, :], -1.0, y_lo[:], ALU.mult, ALU.max)
+
+        def fold(b):
+            nc.vector.tensor_tensor(tops[b][:], pairs[b][:, 0, :, :], pairs[b][:, 1, :, :], ALU.max)
+
+        def margin(b):
+            nc.vector.scalar_tensor_tensor(u[:, b, :], tops[b][:, 0, :], MARGIN, tops[b][:, 1, :], ALU.add, ALU.subtract if b == 0 else ALU.add)
+            if b >= 1:
+                first = 0 if b == 1 else b
+                nc.scalar.activation(e[:, first : b + 1, :], u[:, first : b + 1, :], ACT.Exp)
+
+        for step in range(BLOCKS + 2):
+            if step < BLOCKS:
+                scores(step)
+            if 2 <= step <= BLOCKS:
+                fold(step - 1)
+            if step >= 2:
+                margin(step - 2)
         ec = keep.tile([P, BLOCKS, V], F32, name="ec")
         nc.vector.tensor_scalar(ec[:], e[:], EXP_CAP, None, ALU.min)
         for b in range(BLOCKS):
             lg = keep.tile([P, V], F32, name=f"lg{b}")
             res = keep.tile([P, V], F32, name=f"res{b}")
             nc.scalar.activation(lg[:], ec[:, b, :], ACT.Ln, bias=1.0)
-            nc.vector.tensor_tensor(res[:], u[b][:], lg[:], ALU.max)
+            nc.vector.tensor_tensor(res[:], u[:, b, :], lg[:], ALU.max)
             nc.sync.dma_start(out[b * P : (b + 1) * P, :], res[:])

@@ -81,7 +81,10 @@ def tile_picked_yhard_soft_p_kernel(
             )
         w_q = keep.tile([P, H], U32, name="w_q", align_bytes=64)
         w_s = keep.tile([P, H], U8, name="w_s", align_bytes=64)
-        nc.vector.quantize_mx(out=w_q[:].bitcast(FP8X4), scales=w_s[:], in_=w_bf[:])
+        for half in range(2):
+            words = slice(half * H // 2, (half + 1) * H // 2)
+            values = slice(half * PACK * H // 2, (half + 1) * PACK * H // 2)
+            nc.vector.quantize_mx(out=w_q[:, words].bitcast(FP8X4), scales=w_s[:, words], in_=w_bf[:, values])
 
         h_q, h_s = [], []
         h_bf = []
@@ -138,10 +141,11 @@ def tile_picked_yhard_soft_p_kernel(
             nc.vector.tensor_tensor(tops[b][:], pairs[b][:, 0, :, :], pairs[b][:, 1, :, :], ALU.max)
 
         def margin(b):
-            nc.vector.scalar_tensor_tensor(u[:, b, :], tops[b][:, 0, :], MARGIN, tops[b][:, 1, :], ALU.add, ALU.subtract if b == 0 else ALU.add)
+            engine = nc.gpsimd if b < 2 else nc.vector
+            engine.tensor_tensor(u[:, b, :], tops[b][:, 0, :], tops[b][:, 1, :], ALU.subtract if b == 0 else ALU.add)
             if b >= 1:
                 first = 0 if b == 1 else b
-                nc.scalar.activation(e[:, first : b + 1, :], u[:, first : b + 1, :], ACT.Exp)
+                nc.scalar.activation(e[:, first : b + 1, :], u[:, first : b + 1, :], ACT.Exp, bias=MARGIN)
 
         for step in range(BLOCKS + 2):
             if step < BLOCKS:
@@ -156,5 +160,5 @@ def tile_picked_yhard_soft_p_kernel(
             lg = keep.tile([P, V], F32, name=f"lg{b}")
             res = keep.tile([P, V], F32, name=f"res{b}")
             nc.scalar.activation(lg[:], ec[:, b, :], ACT.Ln, bias=1.0)
-            nc.vector.tensor_tensor(res[:], u[:, b, :], lg[:], ALU.max)
+            nc.vector.scalar_tensor_tensor(res[:], u[:, b, :], MARGIN, lg[:], ALU.add, ALU.max)
             nc.sync.dma_start(out[b * P : (b + 1) * P, :], res[:])

@@ -20,6 +20,7 @@ V = U // D
 BLOCKS = S // P
 MARGIN = 0.3
 EXP_CAP = 2.0 ** 60
+X_PLANE = 4
 
 FLOPS = 2 * K * H * S + 2 * 2 * H * S * U
 
@@ -45,19 +46,19 @@ def tile_picked_yhard_soft_p_kernel(
         nc.gpsimd.memset(es[:, W // 2 :].bitcast(I32), 0)
         nc.vector.memset(xs[:].bitcast(I32), 0)
 
-        def load_scales(tile, scales):
+        def load_scales(tile, scales, first):
             for q in range(4):
-                nc.sync.dma_start(tile[32 * q : 32 * q + 4, :].bitcast(I32), scales[0, 4 * q : 4 * q + 4, :].bitcast(I32))
+                nc.sync.dma_start(tile[32 * q + first : 32 * q + first + 4, :].bitcast(I32), scales[0, 4 * q : 4 * q + 4, :].bitcast(I32))
 
         w_rows = w1.rearrange("(p j) c -> p j c", j=PACK)
         nc.sync.dma_start(offs_t[:], offs)
         nc.sync.dma_start(xw[:], x_words[0].rearrange("p n t -> p (n t)").bitcast(I32))
         nc.sync.dma_start(neg_t[:], neg)
         nc.sync.dma_start(pos_t[:], pos)
-        load_scales(es, e_scales)
+        load_scales(es, e_scales, 0)
         for h in range(2):
             nc.sync.dma_start(w_raw[h][:], w_rows[:, :, h * (H // 2) : (h + 1) * (H // 2)])
-        load_scales(xs, x_scales)
+        load_scales(xs, x_scales, X_PLANE)
         nc.sync.dma_start(ew[:], e_words[0].rearrange("p n t -> p (n t)").bitcast(I32))
 
         xs_g = keep.tile([P, S], U8, name="xs_g", align_bytes=64)
@@ -73,11 +74,11 @@ def tile_picked_yhard_soft_p_kernel(
         nc.vector.tensor_copy(xs_g[:], xs[:].indirect(offs_t[:]))
 
         w_bf = keep.tile([P, PACK * H], BF16, name="w_bf", align_bytes=64)
-        w_view = w_bf[:].rearrange("p (t m j) -> p m t j", t=PACK, j=PACK)
+        w_view = w_bf[:].rearrange("p (t m j) -> p m j t", t=PACK, j=PACK)
         for h in range(2):
             nc.scalar.activation(
                 w_view[:, h * (P // 2) : (h + 1) * (P // 2), :, :],
-                w_raw[h][:].rearrange("p j (m t) -> p m t j", t=PACK), ACT.Copy,
+                w_raw[h][:].rearrange("p j (m t) -> p m j t", t=PACK), ACT.Copy,
             )
         w_q = keep.tile([P, H], U32, name="w_q", align_bytes=64)
         w_s = keep.tile([P, H], U8, name="w_s", align_bytes=64)
@@ -95,7 +96,7 @@ def tile_picked_yhard_soft_p_kernel(
                 wc = slice(t * P, (t + 1) * P)
                 nc.tensor.matmul_mx(
                     out=bank[:, t, :], lhsT=w_q[:, wc].bitcast(FP8X4), lhsT_scale=w_s[:, wc],
-                    rhs=xw_g[:, cols].bitcast(FP8X4), rhs_scale=xs_g[:, cols], start=True, stop=True,
+                    rhs=xw_g[:, cols].bitcast(FP8X4), rhs_scale=xs_g[X_PLANE:, cols], start=True, stop=True,
                 )
             hb = keep.tile([P, P * PACK], BF16, name=f"h_bf{b}", align_bytes=64)
             nc.scalar.copy(hb[:].rearrange("p (n t) -> p n t", t=PACK), bank[:].rearrange("p t n -> p n t"))

@@ -20,7 +20,6 @@ V = U // D
 BLOCKS = S // P
 MARGIN = 0.3
 EXP_CAP = 2.0 ** 60
-X_PLANE = 4
 
 FLOPS = 2 * K * H * S + 2 * 2 * H * S * U
 
@@ -36,44 +35,53 @@ def tile_picked_yhard_soft_p_kernel(
         offs_t = keep.tile([P, S // 16], U16, name="offs_t")
         neg_t = keep.tile([P, U // 16], U16, name="neg_t")
         pos_t = keep.tile([P, U // 16], U16, name="pos_t")
-        xs = keep.tile([P, T], U8, name="xs", align_bytes=64)
+        xs = keep.tile([P, T], U8, name="xs", tag="x_scales_then_w_bf", align_bytes=64)
         es = keep.tile([P, W], U8, name="es", align_bytes=64)
         xw = keep.tile([P, T], I32, name="xw", align_bytes=64)
         ew = keep.tile([P, W], I32, name="ew", tag="e_words_then_h_codes", align_bytes=64)
         w_raw = [keep.tile([P, PACK, H // 2], F32, name=f"w_raw{h}") for h in range(2)]
 
-        nc.vector.memset(es[:, : W // 2].bitcast(I32), 0)
-        nc.gpsimd.memset(es[:, W // 2 :].bitcast(I32), 0)
-        nc.vector.memset(xs[:].bitcast(I32), 0)
+        e_planes = keep.tile([P, 2 * U], U8, name="e_planes", align_bytes=64)
+        x_plane = keep.tile([P, S], U8, name="x_plane", align_bytes=64)
+        nc.gpsimd.memset(xs[:].bitcast(I32), 0)
+        nc.vector.memset(es[:].bitcast(I32), 0)
+        nc.vector.memset(x_plane[:].bitcast(I32), 0)
+        nc.vector.memset(e_planes[:].bitcast(I32), 0)
 
-        def load_scales(tile, scales, first):
+        one = keep.tile([P, 1], F32, name="one")
+        margin_t = keep.tile([P, 1], F32, name="margin_t")
+        nc.gpsimd.memset(one[:], 1.0)
+        nc.scalar.activation(margin_t[:], one[:], ACT.Copy, scale=MARGIN)
+
+        def place_rows(queue, plane, gathered):
             for q in range(4):
-                nc.sync.dma_start(tile[32 * q + first : 32 * q + first + 4, :].bitcast(I32), scales[0, 4 * q : 4 * q + 4, :].bitcast(I32))
+                queue.dma_start(plane[32 * q : 32 * q + 4, :].bitcast(I32), gathered[32 * q : 32 * q + 32 : 8, :].bitcast(I32))
 
         w_rows = w1.rearrange("(p j) c -> p j c", j=PACK)
         nc.sync.dma_start(offs_t[:], offs)
-        nc.sync.dma_start(xw[:], x_words[0].rearrange("p n t -> p (n t)").bitcast(I32))
         nc.sync.dma_start(neg_t[:], neg)
+        nc.sync.dma_start(xs[0:P:8, :].bitcast(I32), x_scales[0].bitcast(I32))
+        nc.sync.dma_start(xw[:], x_words[0].rearrange("p n t -> p (n t)").bitcast(I32))
+        nc.sync.dma_start(es[0:P:8, :].bitcast(I32), e_scales[0].bitcast(I32))
         nc.sync.dma_start(pos_t[:], pos)
-        load_scales(es, e_scales, 0)
         for h in range(2):
             nc.sync.dma_start(w_raw[h][:], w_rows[:, :, h * (H // 2) : (h + 1) * (H // 2)])
-        load_scales(xs, x_scales, X_PLANE)
         nc.sync.dma_start(ew[:], e_words[0].rearrange("p n t -> p (n t)").bitcast(I32))
 
         xs_g = keep.tile([P, S], U8, name="xs_g", align_bytes=64)
         xw_g = keep.tile([P, S], U32, name="xw_g", align_bytes=64)
-        ns_g = keep.tile([P, U], U8, name="ns_g", align_bytes=64)
+        es_g = keep.tile([P, 2 * U], U8, name="es_g", align_bytes=64)
         nw_g = keep.tile([P, U], U32, name="nw_g", align_bytes=64)
-        ps_g = keep.tile([P, U], U8, name="ps_g", align_bytes=64)
         pw_g = keep.tile([P, U], U32, name="pw_g", align_bytes=64)
 
-        nc.vector.tensor_copy(xw_g[:], xw[:].bitcast(U32).indirect(offs_t[:]))
-        nc.vector.tensor_copy(ns_g[:], es[:].indirect(neg_t[:]))
-        nc.vector.tensor_copy(ps_g[:], es[:].indirect(pos_t[:]))
         nc.vector.tensor_copy(xs_g[:], xs[:].indirect(offs_t[:]))
+        place_rows(nc.scalar, x_plane, xs_g)
+        nc.vector.tensor_copy(es_g[:, :U], es[:].indirect(neg_t[:]))
+        nc.vector.tensor_copy(es_g[:, U:], es[:].indirect(pos_t[:]))
+        place_rows(nc.sync, e_planes, es_g)
+        nc.vector.tensor_copy(xw_g[:], xw[:].bitcast(U32).indirect(offs_t[:]))
 
-        w_bf = keep.tile([P, PACK * H], BF16, name="w_bf", align_bytes=64)
+        w_bf = keep.tile([P, PACK * H], BF16, name="w_bf", tag="x_scales_then_w_bf", align_bytes=64)
         w_view = w_bf[:].rearrange("p (t m j) -> p m j t", t=PACK, j=PACK)
         for h in range(2):
             nc.scalar.activation(
@@ -96,7 +104,7 @@ def tile_picked_yhard_soft_p_kernel(
                 wc = slice(t * P, (t + 1) * P)
                 nc.tensor.matmul_mx(
                     out=bank[:, t, :], lhsT=w_q[:, wc].bitcast(FP8X4), lhsT_scale=w_s[:, wc],
-                    rhs=xw_g[:, cols].bitcast(FP8X4), rhs_scale=xs_g[X_PLANE:, cols], start=True, stop=True,
+                    rhs=xw_g[:, cols].bitcast(FP8X4), rhs_scale=x_plane[:, cols], start=True, stop=True,
                 )
             hb = keep.tile([P, P * PACK], BF16, name=f"h_bf{b}", align_bytes=64)
             nc.scalar.copy(hb[:].rearrange("p (n t) -> p n t", t=PACK), bank[:].rearrange("p t n -> p n t"))
@@ -120,10 +128,10 @@ def tile_picked_yhard_soft_p_kernel(
         def scores(b):
             z = psum.tile([P, U], F32, name="z", tag="z")
             y = psum.tile([P, U], F32, name="hy", tag="hy")
-            for bank, words, planes in ((z, nw_g, ns_g), (y, pw_g, ps_g)):
+            for bank, words, planes in ((z, nw_g, e_planes[:, :U]), (y, pw_g, e_planes[:, U:])):
                 nc.tensor.matmul_mx(
                     out=bank[:], lhsT=h_q[b].bitcast(FP8X4), lhsT_scale=h_s[b][:],
-                    rhs=words[:].bitcast(FP8X4), rhs_scale=planes[:], start=True, stop=True,
+                    rhs=words[:].bitcast(FP8X4), rhs_scale=planes, start=True, stop=True,
                 )
             if b == 0:
                 nc.vector.tensor_reduce(tops[b][:, 0, :], z[:].rearrange("p (v d) -> p v d", d=D), AXIS.X, ALU.max)
@@ -146,7 +154,7 @@ def tile_picked_yhard_soft_p_kernel(
             engine.tensor_tensor(u[:, b, :], tops[b][:, 0, :], tops[b][:, 1, :], ALU.subtract if b == 0 else ALU.add)
             if b >= 1:
                 first = 0 if b == 1 else b
-                nc.scalar.activation(e[:, first : b + 1, :], u[:, first : b + 1, :], ACT.Exp, bias=MARGIN)
+                nc.scalar.activation(e[:, first : b + 1, :], u[:, first : b + 1, :], ACT.Exp, bias=margin_t[:])
 
         for step in range(BLOCKS + 2):
             if step < BLOCKS:

@@ -19,6 +19,8 @@ K, T, S, H, D, W, U = 512, 1024, 512, 512, 4, 2048, 512
 V = U // D
 BLOCKS = S // P
 MARGIN = 0.3
+E_CUT = 512
+ROW0 = P - 16
 EXP_CAP = 2.0 ** 60
 
 FLOPS = 2 * K * H * S + 2 * 2 * H * S * U
@@ -30,21 +32,21 @@ def tile_picked_yhard_soft_p_kernel(
     nc = tc.nc
     with ExitStack() as ctx:
         keep = ctx.enter_context(tc.tile_pool(name="keep", bufs=1))
+        shared = ctx.enter_context(tc.tile_pool(name="shared", bufs=1))
         psum = ctx.enter_context(tc.psum_pool(name="psum", bufs=4))
 
         offs_t = keep.tile([P, S // 16], U16, name="offs_t")
         neg_t = keep.tile([P, U // 16], U16, name="neg_t")
         pos_t = keep.tile([P, U // 16], U16, name="pos_t")
-        xs = keep.tile([P, T], U8, name="xs", tag="x_scales_then_w_bf", align_bytes=64)
+        xs = shared.tile([P, T], U8, name="xs", offset=4 * E_CUT, align_bytes=64)
         es = keep.tile([P, W], U8, name="es", align_bytes=64)
         xw = keep.tile([P, T], I32, name="xw", align_bytes=64)
-        ew = keep.tile([P, W], I32, name="ew", tag="e_words_then_h_codes", align_bytes=64)
         w_raw = [keep.tile([P, PACK, H // 2], F32, name=f"w_raw{h}") for h in range(2)]
 
         e_planes = keep.tile([P, 2 * U], U8, name="e_planes", align_bytes=64)
         x_plane = keep.tile([P, S], U8, name="x_plane", align_bytes=64)
-        nc.gpsimd.memset(xs[:].bitcast(I32), 0)
-        nc.vector.memset(es[:].bitcast(I32), 0)
+        nc.vector.memset(xs[:ROW0, :].bitcast(I32), 0)
+        nc.vector.memset(es[:ROW0, :].bitcast(I32), 0)
         nc.vector.memset(x_plane[:].bitcast(I32), 0)
         nc.vector.memset(e_planes[:].bitcast(I32), 0)
 
@@ -53,35 +55,39 @@ def tile_picked_yhard_soft_p_kernel(
         nc.gpsimd.memset(one[:], 1.0)
         nc.scalar.activation(margin_t[:], one[:], ACT.Copy, scale=MARGIN)
 
-        def place_rows(queue, plane, gathered):
+        def place_rows(queues, plane, gathered):
             for q in range(4):
-                queue.dma_start(plane[32 * q : 32 * q + 4, :].bitcast(I32), gathered[32 * q : 32 * q + 32 : 8, :].bitcast(I32))
+                queues[q % len(queues)].dma_start(plane[32 * q : 32 * q + 4, :].bitcast(I32), gathered[ROW0 + 4 * q : ROW0 + 4 * q + 4, :].bitcast(I32))
 
         w_rows = w1.rearrange("(p j) c -> p j c", j=PACK)
         nc.sync.dma_start(offs_t[:], offs)
+        nc.sync.dma_start(xs[ROW0:, :].bitcast(I32), x_scales[0].bitcast(I32))
+        nc.sync.dma_start(w_raw[0][:], w_rows[:, :, : H // 2])
         nc.sync.dma_start(neg_t[:], neg)
-        nc.sync.dma_start(xs[0:P:8, :].bitcast(I32), x_scales[0].bitcast(I32))
-        nc.sync.dma_start(xw[:], x_words[0].rearrange("p n t -> p (n t)").bitcast(I32))
-        nc.sync.dma_start(es[0:P:8, :].bitcast(I32), e_scales[0].bitcast(I32))
+        nc.sync.dma_start(es[ROW0:, :].bitcast(I32), e_scales[0].bitcast(I32))
         nc.sync.dma_start(pos_t[:], pos)
-        for h in range(2):
-            nc.sync.dma_start(w_raw[h][:], w_rows[:, :, h * (H // 2) : (h + 1) * (H // 2)])
-        nc.sync.dma_start(ew[:], e_words[0].rearrange("p n t -> p (n t)").bitcast(I32))
+        nc.sync.dma_start(w_raw[1][:], w_rows[:, :, H // 2 :])
+        nc.sync.dma_start(xw[:], x_words[0].rearrange("p n t -> p (n t)").bitcast(I32))
+
+        ew = shared.tile([P, W], I32, name="ew", offset=0, align_bytes=64)
+        e_rows = e_words[0].rearrange("p n t -> p (n t)").bitcast(I32)
+        nc.sync.dma_start(ew[:, :E_CUT], e_rows[:, :E_CUT])
 
         xs_g = keep.tile([P, S], U8, name="xs_g", align_bytes=64)
         xw_g = keep.tile([P, S], U32, name="xw_g", align_bytes=64)
-        es_g = keep.tile([P, 2 * U], U8, name="es_g", align_bytes=64)
+        es_g = keep.tile([P, 2 * U], U8, name="es_g", tag="e_bytes_then_h_codes", align_bytes=64)
         nw_g = keep.tile([P, U], U32, name="nw_g", align_bytes=64)
         pw_g = keep.tile([P, U], U32, name="pw_g", align_bytes=64)
 
         nc.vector.tensor_copy(xs_g[:], xs[:].indirect(offs_t[:]))
-        place_rows(nc.scalar, x_plane, xs_g)
+        place_rows((nc.sync,), x_plane, xs_g)
+        nc.sync.dma_start(ew[:, E_CUT:], e_rows[:, E_CUT:])
         nc.vector.tensor_copy(es_g[:, :U], es[:].indirect(neg_t[:]))
         nc.vector.tensor_copy(es_g[:, U:], es[:].indirect(pos_t[:]))
-        place_rows(nc.sync, e_planes, es_g)
+        place_rows((nc.sync,), e_planes, es_g)
         nc.vector.tensor_copy(xw_g[:], xw[:].bitcast(U32).indirect(offs_t[:]))
 
-        w_bf = keep.tile([P, PACK * H], BF16, name="w_bf", tag="x_scales_then_w_bf", align_bytes=64)
+        w_bf = keep.tile([P, PACK * H], BF16, name="w_bf", align_bytes=64)
         w_view = w_bf[:].rearrange("p (t m j) -> p m j t", t=PACK, j=PACK)
         for h in range(2):
             nc.scalar.activation(
@@ -112,7 +118,7 @@ def tile_picked_yhard_soft_p_kernel(
 
         nc.vector.tensor_copy(nw_g[:], ew[:].bitcast(U32).indirect(neg_t[:]))
         nc.vector.tensor_copy(pw_g[:], ew[:].bitcast(U32).indirect(pos_t[:]))
-        h_codes = keep.tile([P, S], U32, name="h_codes", tag="e_words_then_h_codes", align_bytes=64)
+        h_codes = keep.tile([P, S], U32, name="h_codes", tag="e_bytes_then_h_codes", align_bytes=64)
         for b in range(BLOCKS):
             hq = h_codes[:, b * P : (b + 1) * P]
             hs = keep.tile([P, P], U8, name=f"h_s{b}", align_bytes=64)

@@ -33,6 +33,7 @@ def tile_picked_yhard_soft_p_kernel(
     with ExitStack() as ctx:
         keep = ctx.enter_context(tc.tile_pool(name="keep", bufs=1))
         shared = ctx.enter_context(tc.tile_pool(name="shared", bufs=1))
+        late = ctx.enter_context(tc.tile_pool(name="late", bufs=1))
         psum = ctx.enter_context(tc.psum_pool(name="psum", bufs=4))
 
         offs_t = keep.tile([P, S // 16], U16, name="offs_t")
@@ -41,7 +42,7 @@ def tile_picked_yhard_soft_p_kernel(
         xs = shared.tile([P, T], U8, name="xs", offset=4 * E_CUT, align_bytes=64)
         es = keep.tile([P, W], U8, name="es", align_bytes=64)
         xw = keep.tile([P, T], I32, name="xw", align_bytes=64)
-        w_raw = [keep.tile([P, PACK, H // 2], F32, name=f"w_raw{h}") for h in range(2)]
+        w_raw = [keep.tile([P, PACK, H // 2], F32, name=f"w_raw{h}", tag=f"w_raw{h}", align_bytes=64) for h in range(2)]
 
         e_planes = keep.tile([P, 2 * U], U8, name="e_planes", align_bytes=64)
         x_plane = keep.tile([P, S], U8, name="x_plane", align_bytes=64)
@@ -61,10 +62,10 @@ def tile_picked_yhard_soft_p_kernel(
 
         w_rows = w1.rearrange("(p j) c -> p j c", j=PACK)
         nc.sync.dma_start(offs_t[:], offs)
-        nc.sync.dma_start(xs[ROW0:, :].bitcast(I32), x_scales[0].bitcast(I32))
+        nc.scalar.dma_start(xs[ROW0:, :].bitcast(I32), x_scales[0].bitcast(I32))
         nc.sync.dma_start(w_raw[0][:], w_rows[:, :, : H // 2])
         nc.sync.dma_start(neg_t[:], neg)
-        nc.sync.dma_start(es[ROW0:, :].bitcast(I32), e_scales[0].bitcast(I32))
+        nc.scalar.dma_start(es[ROW0:, :].bitcast(I32), e_scales[0].bitcast(I32))
         nc.sync.dma_start(pos_t[:], pos)
         nc.sync.dma_start(w_raw[1][:], w_rows[:, :, H // 2 :])
         nc.sync.dma_start(xw[:], x_words[0].rearrange("p n t -> p (n t)").bitcast(I32))
@@ -74,10 +75,8 @@ def tile_picked_yhard_soft_p_kernel(
         nc.sync.dma_start(ew[:, :E_CUT], e_rows[:, :E_CUT])
 
         xs_g = keep.tile([P, S], U8, name="xs_g", align_bytes=64)
-        xw_g = keep.tile([P, S], U32, name="xw_g", align_bytes=64)
-        es_g = keep.tile([P, 2 * U], U8, name="es_g", tag="e_bytes_then_h_codes", align_bytes=64)
+        es_g = late.tile([P, 2 * U], U8, name="es_g", offset=4 * S - U, align_bytes=64)
         nw_g = keep.tile([P, U], U32, name="nw_g", align_bytes=64)
-        pw_g = keep.tile([P, U], U32, name="pw_g", align_bytes=64)
 
         nc.vector.tensor_copy(xs_g[:], xs[:].indirect(offs_t[:]))
         place_rows((nc.sync,), x_plane, xs_g)
@@ -85,8 +84,9 @@ def tile_picked_yhard_soft_p_kernel(
         nc.vector.tensor_copy(es_g[:, :U], es[:].indirect(neg_t[:]))
         nc.vector.tensor_copy(es_g[:, U:], es[:].indirect(pos_t[:]))
         place_rows((nc.sync,), e_planes, es_g)
-        nc.vector.tensor_copy(xw_g[:], xw[:].bitcast(U32).indirect(offs_t[:]))
 
+        xw_first = keep.tile([P, S // 2], U32, name="xw_first", align_bytes=64)
+        nc.vector.tensor_copy(xw_first[:], xw[:].bitcast(U32).indirect(offs_t[:, : S // 32]))
         w_bf = keep.tile([P, PACK * H], BF16, name="w_bf", align_bytes=64)
         w_view = w_bf[:].rearrange("p (t m j) -> p m j t", t=PACK, j=PACK)
         for h in range(2):
@@ -101,6 +101,10 @@ def tile_picked_yhard_soft_p_kernel(
             values = slice(half * PACK * H // 2, (half + 1) * PACK * H // 2)
             nc.vector.quantize_mx(out=w_q[:, words].bitcast(FP8X4), scales=w_s[:, words], in_=w_bf[:, values])
 
+        xw_g = keep.tile([P, S // 2], U32, name="xw_g", tag="w_raw1", align_bytes=64)
+        x_codes = [(xw_first, xw_g)[b // 2][:, (b % 2) * P : (b % 2 + 1) * P] for b in range(BLOCKS)]
+        nc.vector.tensor_copy(xw_g[:], xw[:].bitcast(U32).indirect(offs_t[:, S // 32 :]))
+
         h_q, h_s = [], []
         h_bf = []
         for b in range(BLOCKS):
@@ -110,16 +114,18 @@ def tile_picked_yhard_soft_p_kernel(
                 wc = slice(t * P, (t + 1) * P)
                 nc.tensor.matmul_mx(
                     out=bank[:, t, :], lhsT=w_q[:, wc].bitcast(FP8X4), lhsT_scale=w_s[:, wc],
-                    rhs=xw_g[:, cols].bitcast(FP8X4), rhs_scale=x_plane[:, cols], start=True, stop=True,
+                    rhs=x_codes[b].bitcast(FP8X4), rhs_scale=x_plane[:, cols], start=True, stop=True,
                 )
             hb = keep.tile([P, P * PACK], BF16, name=f"h_bf{b}", align_bytes=64)
             nc.scalar.copy(hb[:].rearrange("p (n t) -> p n t", t=PACK), bank[:].rearrange("p t n -> p n t"))
             h_bf.append(hb)
 
+        h_codes = late.tile([P, S], U32, name="h_codes", offset=0, align_bytes=64)
+        pw_g = late.tile([P, U], U32, name="pw_g", offset=4 * S, align_bytes=64)
         nc.vector.tensor_copy(nw_g[:], ew[:].bitcast(U32).indirect(neg_t[:]))
-        nc.vector.tensor_copy(pw_g[:], ew[:].bitcast(U32).indirect(pos_t[:]))
-        h_codes = keep.tile([P, S], U32, name="h_codes", tag="e_bytes_then_h_codes", align_bytes=64)
         for b in range(BLOCKS):
+            if b == 2:
+                nc.vector.tensor_copy(pw_g[:], ew[:].bitcast(U32).indirect(pos_t[:]))
             hq = h_codes[:, b * P : (b + 1) * P]
             hs = keep.tile([P, P], U8, name=f"h_s{b}", align_bytes=64)
             nc.vector.quantize_mx(out=hq.bitcast(FP8X4), scales=hs[:], in_=h_bf[b][:])
@@ -128,28 +134,27 @@ def tile_picked_yhard_soft_p_kernel(
 
         u = keep.tile([P, BLOCKS, V], F32, name="u")
         e = keep.tile([P, BLOCKS, V], F32, name="e")
-        pairs = [None] + [keep.tile([P, 2, 2, V], F32, name=f"pairs{b}") for b in range(1, BLOCKS)]
+        pairs = [keep.tile([P, 2, 2, V], F32, name=f"pairs{b}") for b in range(BLOCKS)]
         tops = [keep.tile([P, 2, V], F32, name=f"tops{b}") for b in range(BLOCKS)]
 
-        def scores(b):
-            z = psum.tile([P, U], F32, name="z", tag="z")
-            y = psum.tile([P, U], F32, name="hy", tag="hy")
-            for bank, words, planes in ((z, nw_g, e_planes[:, :U]), (y, pw_g, e_planes[:, U:])):
-                nc.tensor.matmul_mx(
-                    out=bank[:], lhsT=h_q[b].bitcast(FP8X4), lhsT_scale=h_s[b][:],
-                    rhs=words[:].bitcast(FP8X4), rhs_scale=planes, start=True, stop=True,
-                )
-            if b == 0:
-                nc.vector.tensor_reduce(tops[b][:, 0, :], z[:].rearrange("p (v d) -> p v d", d=D), AXIS.X, ALU.max)
-                nc.vector.tensor_reduce(tops[b][:, 1, :], y[:].rearrange("p (v d) -> p v d", d=D), AXIS.X, ALU.min)
-                return
-            z_d = z[:].rearrange("p (v d) -> p d v", d=D)
-            y_d = y[:].rearrange("p (v d) -> p d v", d=D)
+        def product(b, tag, words, planes):
+            bank = psum.tile([P, U], F32, name=tag, tag=tag)
+            nc.tensor.matmul_mx(
+                out=bank[:], lhsT=h_q[b].bitcast(FP8X4), lhsT_scale=h_s[b][:],
+                rhs=words[:].bitcast(FP8X4), rhs_scale=planes, start=True, stop=True,
+            )
+            return bank[:].rearrange("p (v d) -> p d v", d=D)
+
+        def negatives(b):
+            z_d = product(b, "z", nw_g, e_planes[:, :U])
             z_lo = keep.tile([P, 2, V], F32, name=f"z_lo{b}")
-            y_lo = keep.tile([P, 2, V], F32, name=f"y_lo{b}")
             nc.scalar.copy(z_lo[:], z_d[:, 0:2, :])
-            nc.scalar.activation(y_lo[:], y_d[:, 0:2, :], ACT.Copy, scale=-1.0)
             nc.vector.tensor_tensor(pairs[b][:, :, 0, :], z_d[:, 2:4, :], z_lo[:], ALU.max)
+
+        def positives(b):
+            y_d = product(b, "hy", pw_g, e_planes[:, U:])
+            y_lo = keep.tile([P, 2, V], F32, name=f"y_lo{b}")
+            nc.scalar.activation(y_lo[:], y_d[:, 0:2, :], ACT.Copy, scale=-1.0)
             nc.vector.scalar_tensor_tensor(pairs[b][:, :, 1, :], y_d[:, 2:4, :], -1.0, y_lo[:], ALU.mult, ALU.max)
 
         def fold(b):
@@ -157,18 +162,29 @@ def tile_picked_yhard_soft_p_kernel(
 
         def margin(b):
             engine = nc.gpsimd if b < 2 else nc.vector
-            engine.tensor_tensor(u[:, b, :], tops[b][:, 0, :], tops[b][:, 1, :], ALU.subtract if b == 0 else ALU.add)
-            if b >= 1:
-                first = 0 if b == 1 else b
-                nc.scalar.activation(e[:, first : b + 1, :], u[:, first : b + 1, :], ACT.Exp, bias=margin_t[:])
+            engine.tensor_tensor(u[:, b, :], tops[b][:, 0, :], tops[b][:, 1, :], ALU.add)
 
-        for step in range(BLOCKS + 2):
-            if step < BLOCKS:
-                scores(step)
-            if 2 <= step <= BLOCKS:
-                fold(step - 1)
-            if step >= 2:
-                margin(step - 2)
+        def exponential(first, last):
+            nc.scalar.activation(e[:, first:last, :], u[:, first:last, :], ACT.Exp, bias=margin_t[:])
+
+        negatives(0)
+        negatives(1)
+        positives(0)
+        positives(1)
+        fold(0)
+        negatives(2)
+        fold(1)
+        margin(0)
+        positives(2)
+        negatives(3)
+        margin(1)
+        positives(3)
+        fold(2)
+        fold(3)
+        exponential(0, 2)
+        for b in range(2, BLOCKS):
+            margin(b)
+            exponential(b, b + 1)
         ec = keep.tile([P, BLOCKS, V], F32, name="ec")
         nc.vector.tensor_scalar(ec[:], e[:], EXP_CAP, None, ALU.min)
         for b in range(BLOCKS):

@@ -1,6 +1,7 @@
 from contextlib import ExitStack
 
 import concourse.mybir as mybir
+from concourse.masks import make_identity
 
 F32 = mybir.dt.float32
 BF16 = mybir.dt.bfloat16
@@ -53,7 +54,9 @@ def tile_picked_yhard_soft_p_kernel(
 
         one = keep.tile([P, 1], F32, name="one")
         margin_t = keep.tile([P, 1], F32, name="margin_t")
+        ident = keep.tile([P, P], F32, name="ident")
         nc.gpsimd.memset(one[:], 1.0)
+        make_identity(nc, ident[:])
         nc.scalar.activation(margin_t[:], one[:], ACT.Copy, scale=MARGIN)
 
         def place_rows(queues, plane, gathered):
@@ -132,10 +135,12 @@ def tile_picked_yhard_soft_p_kernel(
             h_q.append(hq)
             h_s.append(hs)
 
-        u = keep.tile([P, BLOCKS, V], F32, name="u")
-        e = keep.tile([P, BLOCKS, V], F32, name="e")
-        pairs = [keep.tile([P, 2, 2, V], F32, name=f"pairs{b}") for b in range(BLOCKS)]
-        tops = [keep.tile([P, 2, V], F32, name=f"tops{b}") for b in range(BLOCKS)]
+        last = BLOCKS - 1
+        z_pairs = keep.tile([P, BLOCKS, 2, V], F32, name="z_pairs")
+        z_top = keep.tile([P, BLOCKS, V], F32, name="z_top")
+        y_pairs = keep.tile([P, BLOCKS, 2, V], F32, name="y_pairs")
+        u_pairs = keep.tile([P, 2, V], F32, name="u_pairs")
+        e_pairs = keep.tile([P, BLOCKS, 2, V], F32, name="e_pairs")
 
         def product(b, tag, words, planes):
             bank = psum.tile([P, U], F32, name=tag, tag=tag)
@@ -149,47 +154,68 @@ def tile_picked_yhard_soft_p_kernel(
             z_d = product(b, "z", nw_g, e_planes[:, :U])
             z_lo = keep.tile([P, 2, V], F32, name=f"z_lo{b}")
             nc.scalar.copy(z_lo[:], z_d[:, 0:2, :])
-            nc.vector.tensor_tensor(pairs[b][:, :, 0, :], z_d[:, 2:4, :], z_lo[:], ALU.max)
+            nc.vector.tensor_tensor(z_pairs[:, b], z_d[:, 2:4, :], z_lo[:], ALU.max)
 
         def positives(b):
             y_d = product(b, "hy", pw_g, e_planes[:, U:])
-            y_lo = keep.tile([P, 2, V], F32, name=f"y_lo{b}")
+            y_lo = keep.tile([P, 2, V], F32, name=f"y_lo{b}", tag=f"y_lo{b}")
             nc.scalar.activation(y_lo[:], y_d[:, 0:2, :], ACT.Copy, scale=-1.0)
-            nc.vector.scalar_tensor_tensor(pairs[b][:, :, 1, :], y_d[:, 2:4, :], -1.0, y_lo[:], ALU.mult, ALU.max)
+            return y_d, y_lo
 
-        def fold(b):
-            nc.vector.tensor_tensor(tops[b][:], pairs[b][:, 0, :, :], pairs[b][:, 1, :, :], ALU.max)
+        def pair_up(b, y_d, y_lo, first, end):
+            nc.vector.scalar_tensor_tensor(
+                y_pairs[:, b, first:end, :], y_d[:, 2 + first : 2 + end, :], -1.0, y_lo[:, first:end, :], ALU.mult, ALU.max
+            )
+
+        def fold(first, end):
+            nc.vector.tensor_tensor(z_top[:, first:end, :], z_pairs[:, first:end, 0, :], z_pairs[:, first:end, 1, :], ALU.max)
 
         def margin(b):
-            engine = nc.gpsimd if b < 2 else nc.vector
-            engine.tensor_tensor(u[:, b, :], tops[b][:, 0, :], tops[b][:, 1, :], ALU.add)
-
-        def exponential(first, last):
-            nc.scalar.activation(e[:, first:last, :], u[:, first:last, :], ACT.Exp, bias=margin_t[:])
+            bank = psum.tile([V, PACK, P], F32, name="z", tag="z")
+            for i in range(2):
+                nc.tensor.matmul(bank[:, i, :], z_top[:, b, :], ident[:], start=True, stop=False, is_transpose=True)
+                nc.tensor.matmul(bank[:, i, :], y_pairs[:, b, i, :], ident[:], start=False, stop=True, is_transpose=True)
+            nc.scalar.activation(e_pairs[:, b], bank[:, 0:2, :], ACT.Exp, bias=margin_t[:])
 
         negatives(0)
         negatives(1)
-        positives(0)
-        positives(1)
-        fold(0)
+        pair_up(0, *positives(0), 0, 2)
+        fold(0, 2)
+        pair_up(1, *positives(1), 0, 2)
         negatives(2)
-        fold(1)
-        margin(0)
-        positives(2)
+        pair_up(2, *positives(2), 0, 2)
         negatives(3)
-        margin(1)
-        positives(3)
-        fold(2)
-        fold(3)
-        exponential(0, 2)
-        for b in range(2, BLOCKS):
+        fold(2, 3)
+        y_last = positives(last)
+        pair_up(last, *y_last, 0, 1)
+        fold(last, BLOCKS)
+        pair_up(last, *y_last, 1, 2)
+        for b in range(last):
             margin(b)
-            exponential(b, b + 1)
-        ec = keep.tile([P, BLOCKS, V], F32, name="ec")
-        nc.vector.tensor_scalar(ec[:], e[:], EXP_CAP, None, ALU.min)
-        for b in range(BLOCKS):
+        for i in range(2):
+            nc.vector.tensor_tensor(u_pairs[:, i, :], y_pairs[:, last, i, :], z_top[:, last, :], ALU.add)
+            nc.scalar.activation(e_pairs[:, last, i, :], u_pairs[:, i, :], ACT.Exp, bias=margin_t[:])
+
+        e = [keep.tile([V, 2, P], F32, name=f"e{a}", tag=f"y_lo{last - a}") for a in range(2)]
+        ec = keep.tile([V, BLOCKS, P], F32, name="ec")
+        u = keep.tile([P, BLOCKS, V], F32, name="u")
+        y_top = keep.tile([P, last, V], F32, name="y_top")
+        for a in range(2):
+            both = slice(2 * a, 2 * a + 2)
+            nc.vector.tensor_tensor(e[a][:], e_pairs[:, both, 0, :], e_pairs[:, both, 1, :], ALU.max)
+            if a == 0:
+                nc.vector.tensor_tensor(y_top[:], y_pairs[:, :last, 0, :], y_pairs[:, :last, 1, :], ALU.max)
+            nc.vector.tensor_scalar(ec[:, both, :], e[a][:], EXP_CAP, None, ALU.min)
+        nc.vector.tensor_tensor(u[:, :last, :], z_top[:, :last, :], y_top[:], ALU.add)
+        nc.vector.tensor_tensor(u[:, last, :], u_pairs[:, 0, :], u_pairs[:, 1, :], ALU.max)
+        for b in (0, 1, last, 2):
             lg = keep.tile([P, V], F32, name=f"lg{b}")
             res = keep.tile([P, V], F32, name=f"res{b}")
-            nc.scalar.activation(lg[:], ec[:, b, :], ACT.Ln, bias=1.0)
+            if b < last:
+                back = psum.tile([P, PACK, V], F32, name="hy", tag="hy")
+                nc.tensor.transpose(back[:, 0, :], ec[:, b, :], ident[:])
+                nc.scalar.activation(lg[:], back[:, 0, :], ACT.Ln, bias=1.0)
+            else:
+                nc.scalar.activation(lg[:], ec[:, b, :], ACT.Ln, bias=1.0)
             nc.vector.scalar_tensor_tensor(res[:], u[:, b, :], MARGIN, lg[:], ALU.add, ALU.max)
             nc.sync.dma_start(out[b * P : (b + 1) * P, :], res[:])

@@ -1,3 +1,4 @@
+import math
 from contextlib import ExitStack
 
 import concourse.mybir as mybir
@@ -22,7 +23,7 @@ BLOCKS = S // P
 MARGIN = 0.3
 E_CUT = 512
 ROW0 = P - 16
-EXP_CAP = 2.0 ** 60
+LOG_CAP = 44.0
 
 FLOPS = 2 * K * H * S + 2 * 2 * H * S * U
 
@@ -53,11 +54,11 @@ def tile_picked_yhard_soft_p_kernel(
         nc.vector.memset(e_planes[:].bitcast(I32), 0)
 
         one = keep.tile([P, 1], F32, name="one")
-        margin_t = keep.tile([P, 1], F32, name="margin_t")
+        zero = keep.tile([P, 1], F32, name="zero", tag="zero")
         ident = keep.tile([P, P], F32, name="ident")
         nc.gpsimd.memset(one[:], 1.0)
         make_identity(nc, ident[:])
-        nc.scalar.activation(margin_t[:], one[:], ACT.Copy, scale=MARGIN)
+        nc.scalar.activation(zero[:], one[:], ACT.Copy, bias=-1.0)
 
         def place_rows(queues, plane, gathered):
             for q in range(4):
@@ -138,7 +139,8 @@ def tile_picked_yhard_soft_p_kernel(
         last = BLOCKS - 1
         z_pairs = keep.tile([P, BLOCKS, 2, V], F32, name="z_pairs")
         z_top = keep.tile([P, BLOCKS, V], F32, name="z_top")
-        y_pairs = keep.tile([P, BLOCKS, 2, V], F32, name="y_pairs")
+        y_pairs = keep.tile([P, last, 2, V], F32, name="y_pairs")
+        y_last_pairs = [keep.tile([P, V], F32, name=f"y_last{i}", tag=f"y_last{i}") for i in range(2)]
         u_pairs = keep.tile([P, 2, V], F32, name="u_pairs")
         e_pairs = keep.tile([P, BLOCKS, 2, V], F32, name="e_pairs")
 
@@ -153,8 +155,8 @@ def tile_picked_yhard_soft_p_kernel(
         def negatives(b):
             z_d = product(b, "z", nw_g, e_planes[:, :U])
             z_lo = keep.tile([P, 2, V], F32, name=f"z_lo{b}")
-            nc.scalar.copy(z_lo[:], z_d[:, 0:2, :])
-            nc.vector.tensor_tensor(z_pairs[:, b], z_d[:, 2:4, :], z_lo[:], ALU.max)
+            nc.scalar.activation(z_lo[:], z_d[:, 0:2, :], ACT.Copy, bias=MARGIN)
+            nc.vector.scalar_tensor_tensor(z_pairs[:, b], z_d[:, 2:4, :], MARGIN, z_lo[:], ALU.add, ALU.max)
 
         def positives(b):
             y_d = product(b, "hy", pw_g, e_planes[:, U:])
@@ -162,10 +164,11 @@ def tile_picked_yhard_soft_p_kernel(
             nc.scalar.activation(y_lo[:], y_d[:, 0:2, :], ACT.Copy, scale=-1.0)
             return y_d, y_lo
 
-        def pair_up(b, y_d, y_lo, first, end):
-            nc.vector.scalar_tensor_tensor(
-                y_pairs[:, b, first:end, :], y_d[:, 2 + first : 2 + end, :], -1.0, y_lo[:, first:end, :], ALU.mult, ALU.max
-            )
+        def pair_up(b, y_d, y_lo):
+            nc.vector.scalar_tensor_tensor(y_pairs[:, b], y_d[:, 2:4, :], -1.0, y_lo[:], ALU.mult, ALU.max)
+
+        def pair_up_last(i, y_d, y_lo):
+            nc.vector.scalar_tensor_tensor(y_last_pairs[i][:], y_d[:, 2 + i, :], -1.0, y_lo[:, i, :], ALU.mult, ALU.max)
 
         def fold(first, end):
             nc.vector.tensor_tensor(z_top[:, first:end, :], z_pairs[:, first:end, 0, :], z_pairs[:, first:end, 1, :], ALU.max)
@@ -175,37 +178,37 @@ def tile_picked_yhard_soft_p_kernel(
             for i in range(2):
                 nc.tensor.matmul(bank[:, i, :], z_top[:, b, :], ident[:], start=True, stop=False, is_transpose=True)
                 nc.tensor.matmul(bank[:, i, :], y_pairs[:, b, i, :], ident[:], start=False, stop=True, is_transpose=True)
-            nc.scalar.activation(e_pairs[:, b], bank[:, 0:2, :], ACT.Exp, bias=margin_t[:])
+            nc.scalar.activation(e_pairs[:, b], bank[:, 0:2, :], ACT.Exp, bias=zero[:])
 
         negatives(0)
         negatives(1)
-        pair_up(0, *positives(0), 0, 2)
+        pair_up(0, *positives(0))
         fold(0, 2)
-        pair_up(1, *positives(1), 0, 2)
+        pair_up(1, *positives(1))
         negatives(2)
-        pair_up(2, *positives(2), 0, 2)
+        pair_up(2, *positives(2))
         negatives(3)
         fold(2, 3)
         y_last = positives(last)
-        pair_up(last, *y_last, 0, 1)
+        pair_up_last(0, *y_last)
         fold(last, BLOCKS)
-        pair_up(last, *y_last, 1, 2)
+        pair_up_last(1, *y_last)
         for b in range(last):
             margin(b)
         for i in range(2):
-            nc.vector.tensor_tensor(u_pairs[:, i, :], y_pairs[:, last, i, :], z_top[:, last, :], ALU.add)
-            nc.scalar.activation(e_pairs[:, last, i, :], u_pairs[:, i, :], ACT.Exp, bias=margin_t[:])
+            nc.vector.tensor_tensor(u_pairs[:, i, :], y_last_pairs[i][:], z_top[:, last, :], ALU.add)
+            nc.scalar.activation(e_pairs[:, last, i, :], u_pairs[:, i, :], ACT.Exp, bias=zero[:])
 
+        cap = keep.tile([P, 1], F32, name="cap", tag="zero")
+        nc.scalar.activation(cap[:], one[:], ACT.Ln, scale=math.exp(LOG_CAP))
         e = [keep.tile([V, 2, P], F32, name=f"e{a}", tag=f"y_lo{last - a}") for a in range(2)]
-        ec = keep.tile([V, BLOCKS, P], F32, name="ec")
         u = keep.tile([P, BLOCKS, V], F32, name="u")
         y_top = keep.tile([P, last, V], F32, name="y_top")
         for a in range(2):
             both = slice(2 * a, 2 * a + 2)
             nc.vector.tensor_tensor(e[a][:], e_pairs[:, both, 0, :], e_pairs[:, both, 1, :], ALU.max)
             if a == 0:
-                nc.vector.tensor_tensor(y_top[:], y_pairs[:, :last, 0, :], y_pairs[:, :last, 1, :], ALU.max)
-            nc.vector.tensor_scalar(ec[:, both, :], e[a][:], EXP_CAP, None, ALU.min)
+                nc.vector.tensor_tensor(y_top[:], y_pairs[:, :, 0, :], y_pairs[:, :, 1, :], ALU.max)
         nc.vector.tensor_tensor(u[:, :last, :], z_top[:, :last, :], y_top[:], ALU.add)
         nc.vector.tensor_tensor(u[:, last, :], u_pairs[:, 0, :], u_pairs[:, 1, :], ALU.max)
         for b in (0, 1, last, 2):
@@ -213,9 +216,9 @@ def tile_picked_yhard_soft_p_kernel(
             res = keep.tile([P, V], F32, name=f"res{b}")
             if b < last:
                 back = psum.tile([P, PACK, V], F32, name="hy", tag="hy")
-                nc.tensor.transpose(back[:, 0, :], ec[:, b, :], ident[:])
+                nc.tensor.transpose(back[:, 0, :], e[b // 2][:, b % 2, :], ident[:])
                 nc.scalar.activation(lg[:], back[:, 0, :], ACT.Ln, bias=1.0)
             else:
-                nc.scalar.activation(lg[:], ec[:, b, :], ACT.Ln, bias=1.0)
-            nc.vector.scalar_tensor_tensor(res[:], u[:, b, :], MARGIN, lg[:], ALU.add, ALU.max)
+                nc.scalar.activation(lg[:], e[b // 2][:, b % 2, :], ACT.Ln, bias=1.0)
+            nc.vector.scalar_tensor_tensor(res[:], lg[:], cap[:], u[:, b, :], ALU.min, ALU.max)
             nc.sync.dma_start(out[b * P : (b + 1) * P, :], res[:])

@@ -1,4 +1,3 @@
-import math
 from contextlib import ExitStack
 
 import concourse.mybir as mybir
@@ -53,12 +52,8 @@ def tile_picked_yhard_soft_p_kernel(
         nc.vector.memset(x_plane[:].bitcast(I32), 0)
         nc.vector.memset(e_planes[:].bitcast(I32), 0)
 
-        one = keep.tile([P, 1], F32, name="one")
-        zero = keep.tile([P, 1], F32, name="zero", tag="zero")
         ident = keep.tile([P, P], F32, name="ident")
-        nc.gpsimd.memset(one[:], 1.0)
         make_identity(nc, ident[:])
-        nc.scalar.activation(zero[:], one[:], ACT.Copy, bias=-1.0)
 
         def place_rows(queues, plane, gathered):
             for q in range(4):
@@ -178,7 +173,7 @@ def tile_picked_yhard_soft_p_kernel(
             for i in range(2):
                 nc.tensor.matmul(bank[:, i, :], z_top[:, b, :], ident[:], start=True, stop=False, is_transpose=True)
                 nc.tensor.matmul(bank[:, i, :], y_pairs[:, b, i, :], ident[:], start=False, stop=True, is_transpose=True)
-            nc.scalar.activation(e_pairs[:, b], bank[:, 0:2, :], ACT.Exp, bias=zero[:])
+            nc.scalar.activation(e_pairs[:, b], bank[:, 0:2, :], ACT.Exp)
 
         negatives(0)
         negatives(1)
@@ -197,20 +192,16 @@ def tile_picked_yhard_soft_p_kernel(
             margin(b)
         for i in range(2):
             nc.vector.tensor_tensor(u_pairs[:, i, :], y_last_pairs[i][:], z_top[:, last, :], ALU.add)
-            nc.scalar.activation(e_pairs[:, last, i, :], u_pairs[:, i, :], ACT.Exp, bias=zero[:])
+            nc.scalar.activation(e_pairs[:, last, i, :], u_pairs[:, i, :], ACT.Exp)
 
-        cap = keep.tile([P, 1], F32, name="cap", tag="zero")
-        nc.scalar.activation(cap[:], one[:], ACT.Ln, scale=math.exp(LOG_CAP))
-        e = [keep.tile([V, 2, P], F32, name=f"e{a}", tag=f"y_lo{last - a}") for a in range(2)]
         u = keep.tile([P, BLOCKS, V], F32, name="u")
-        y_top = keep.tile([P, last, V], F32, name="y_top")
-        for a in range(2):
-            both = slice(2 * a, 2 * a + 2)
-            nc.vector.tensor_tensor(e[a][:], e_pairs[:, both, 0, :], e_pairs[:, both, 1, :], ALU.max)
-            if a == 0:
-                nc.vector.tensor_tensor(y_top[:], y_pairs[:, :, 0, :], y_pairs[:, :, 1, :], ALU.max)
-        nc.vector.tensor_tensor(u[:, :last, :], z_top[:, :last, :], y_top[:], ALU.add)
+        y_top = keep.tile([P, last, V], F32, name="y_top", tag="y_top")
+        e = [keep.tile([V, 2, P], F32, name=f"e{a}", tag=("y_lo3", "y_top")[a]) for a in range(2)]
+        nc.vector.tensor_tensor(e[0][:], e_pairs[:, 0:2, 0, :], e_pairs[:, 0:2, 1, :], ALU.max)
+        nc.vector.tensor_tensor(y_top[:], y_pairs[:, :, 0, :], y_pairs[:, :, 1, :], ALU.max)
         nc.vector.tensor_tensor(u[:, last, :], u_pairs[:, 0, :], u_pairs[:, 1, :], ALU.max)
+        nc.vector.tensor_tensor(u[:, :last, :], z_top[:, :last, :], y_top[:], ALU.add)
+        nc.vector.tensor_tensor(e[1][:], e_pairs[:, 2:4, 0, :], e_pairs[:, 2:4, 1, :], ALU.max)
         for b in (0, 1, last, 2):
             lg = keep.tile([P, V], F32, name=f"lg{b}")
             res = keep.tile([P, V], F32, name=f"res{b}")
@@ -220,5 +211,5 @@ def tile_picked_yhard_soft_p_kernel(
                 nc.scalar.activation(lg[:], back[:, 0, :], ACT.Ln, bias=1.0)
             else:
                 nc.scalar.activation(lg[:], e[b // 2][:, b % 2, :], ACT.Ln, bias=1.0)
-            nc.vector.scalar_tensor_tensor(res[:], lg[:], cap[:], u[:, b, :], ALU.min, ALU.max)
+            nc.vector.scalar_tensor_tensor(res[:], lg[:], LOG_CAP, u[:, b, :], ALU.min, ALU.max)
             nc.sync.dma_start(out[b * P : (b + 1) * P, :], res[:])

@@ -35,6 +35,7 @@ def tile_picked_yhard_soft_p_kernel(
         keep = ctx.enter_context(tc.tile_pool(name="keep", bufs=1))
         shared = ctx.enter_context(tc.tile_pool(name="shared", bufs=1))
         late = ctx.enter_context(tc.tile_pool(name="late", bufs=1))
+        tail = ctx.enter_context(tc.tile_pool(name="tail", bufs=1))
         psum = ctx.enter_context(tc.psum_pool(name="psum", bufs=4))
 
         offs_t = keep.tile([P, S // 16], U16, name="offs_t")
@@ -123,7 +124,7 @@ def tile_picked_yhard_soft_p_kernel(
         pw_g = late.tile([P, U], U32, name="pw_g", offset=4 * S, align_bytes=64)
         nc.vector.tensor_copy(nw_g[:], ew[:].bitcast(U32).indirect(neg_t[:]))
         for b in range(BLOCKS):
-            if b == 2:
+            if b == 3:
                 nc.vector.tensor_copy(pw_g[:], ew[:].bitcast(U32).indirect(pos_t[:]))
             hq = h_codes[:, b * P : (b + 1) * P]
             hs = keep.tile([P, P], U8, name=f"h_s{b}", align_bytes=64)
@@ -135,7 +136,7 @@ def tile_picked_yhard_soft_p_kernel(
         z_pairs = keep.tile([P, BLOCKS, 2, V], F32, name="z_pairs")
         z_top = keep.tile([P, BLOCKS, V], F32, name="z_top")
         y_pairs = keep.tile([P, last, 2, V], F32, name="y_pairs")
-        y_last_pairs = [keep.tile([P, V], F32, name=f"y_last{i}", tag=f"y_last{i}") for i in range(2)]
+        y_last_pairs = [tail.tile([P, V], F32, name="y_last0", offset=0), keep.tile([P, V], F32, name="y_last1")]
         u_pairs = keep.tile([P, 2, V], F32, name="u_pairs")
         e_pairs = keep.tile([P, BLOCKS, 2, V], F32, name="e_pairs")
 
@@ -177,13 +178,13 @@ def tile_picked_yhard_soft_p_kernel(
 
         negatives(0)
         negatives(1)
-        pair_up(0, *positives(0))
-        fold(0, 2)
-        pair_up(1, *positives(1))
         negatives(2)
+        fold(0, 2)
+        pair_up(0, *positives(0))
+        fold(2, 3)
+        pair_up(1, *positives(1))
         pair_up(2, *positives(2))
         negatives(3)
-        fold(2, 3)
         y_last = positives(last)
         pair_up_last(0, *y_last)
         fold(last, BLOCKS)
@@ -195,21 +196,22 @@ def tile_picked_yhard_soft_p_kernel(
             nc.scalar.activation(e_pairs[:, last, i, :], u_pairs[:, i, :], ACT.Exp)
 
         u = keep.tile([P, BLOCKS, V], F32, name="u")
-        y_top = keep.tile([P, last, V], F32, name="y_top", tag="y_top")
-        e = [keep.tile([V, 2, P], F32, name=f"e{a}", tag=("y_lo3", "y_top")[a]) for a in range(2)]
+        y_top = tail.tile([P, last, V], F32, name="y_top", offset=0)
+        e = [keep.tile([V, 2, P], F32, name=f"e{a}", tag=f"y_lo{last - a}") for a in range(2)]
         nc.vector.tensor_tensor(e[0][:], e_pairs[:, 0:2, 0, :], e_pairs[:, 0:2, 1, :], ALU.max)
         nc.vector.tensor_tensor(y_top[:], y_pairs[:, :, 0, :], y_pairs[:, :, 1, :], ALU.max)
+        nc.vector.tensor_tensor(e[1][:], e_pairs[:, 2:4, 0, :], e_pairs[:, 2:4, 1, :], ALU.max)
         nc.vector.tensor_tensor(u[:, last, :], u_pairs[:, 0, :], u_pairs[:, 1, :], ALU.max)
         nc.vector.tensor_tensor(u[:, :last, :], z_top[:, :last, :], y_top[:], ALU.add)
-        nc.vector.tensor_tensor(e[1][:], e_pairs[:, 2:4, 0, :], e_pairs[:, 2:4, 1, :], ALU.max)
-        for b in (0, 1, last, 2):
-            lg = keep.tile([P, V], F32, name=f"lg{b}")
+        logs = tail.tile([P, BLOCKS, V], F32, name="logs", offset=0)
+        for b in (last, 0, 1, 2):
+            lg = logs[:, b, :]
             res = keep.tile([P, V], F32, name=f"res{b}")
             if b < last:
                 back = psum.tile([P, PACK, V], F32, name="hy", tag="hy")
                 nc.tensor.transpose(back[:, 0, :], e[b // 2][:, b % 2, :], ident[:])
-                nc.scalar.activation(lg[:], back[:, 0, :], ACT.Ln, bias=1.0)
+                nc.scalar.activation(lg, back[:, 0, :], ACT.Ln, bias=1.0)
             else:
-                nc.scalar.activation(lg[:], e[b // 2][:, b % 2, :], ACT.Ln, bias=1.0)
-            nc.vector.scalar_tensor_tensor(res[:], lg[:], LOG_CAP, u[:, b, :], ALU.min, ALU.max)
+                nc.scalar.activation(lg, e[b // 2][:, b % 2, :], ACT.Ln, bias=1.0)
+            nc.vector.scalar_tensor_tensor(res[:], lg, LOG_CAP, u[:, b, :], ALU.min, ALU.max)
             nc.sync.dma_start(out[b * P : (b + 1) * P, :], res[:])

@@ -50,6 +50,10 @@ def tile_picked_yhard_soft_p_kernel(
         x_plane = keep.tile([P, S], U8, name="x_plane", align_bytes=64)
         nc.vector.memset(xs[:ROW0, :].bitcast(I32), 0)
         nc.vector.memset(es[:ROW0, :].bitcast(I32), 0)
+        zero = keep.tile([P, 1], F32, name="zero")
+        one = keep.tile([P, 1], F32, name="one")
+        nc.vector.memset(zero[:], 0.0)
+        nc.vector.tensor_scalar(one[:], zero[:], 1.0, None, ALU.add)
         nc.vector.memset(x_plane[:].bitcast(I32), 0)
         nc.vector.memset(e_planes[:].bitcast(I32), 0)
 
@@ -61,10 +65,10 @@ def tile_picked_yhard_soft_p_kernel(
                 queues[q % len(queues)].dma_start(plane[32 * q : 32 * q + 4, :].bitcast(I32), gathered[ROW0 + 4 * q : ROW0 + 4 * q + 4, :].bitcast(I32))
 
         w_rows = w1.rearrange("(p j) c -> p j c", j=PACK)
-        nc.sync.dma_start(offs_t[:], offs)
         nc.scalar.dma_start(xs[ROW0:, :].bitcast(I32), x_scales[0].bitcast(I32))
-        nc.sync.dma_start(w_raw[0][:], w_rows[:, :, : H // 2])
+        nc.sync.dma_start(offs_t[:], offs)
         nc.sync.dma_start(neg_t[:], neg)
+        nc.sync.dma_start(w_raw[0][:], w_rows[:, :, : H // 2])
         nc.scalar.dma_start(es[ROW0:, :].bitcast(I32), e_scales[0].bitcast(I32))
         nc.sync.dma_start(pos_t[:], pos)
         nc.sync.dma_start(w_raw[1][:], w_rows[:, :, H // 2 :])
@@ -210,8 +214,8 @@ def tile_picked_yhard_soft_p_kernel(
             if b < last:
                 back = psum.tile([P, PACK, V], F32, name="hy", tag="hy")
                 nc.tensor.transpose(back[:, 0, :], e[b // 2][:, b % 2, :], ident[:])
-                nc.scalar.activation(lg, back[:, 0, :], ACT.Ln, bias=1.0)
+                nc.scalar.activation(lg, back[:, 0, :], ACT.Ln, bias=one[:])
             else:
-                nc.scalar.activation(lg, e[b // 2][:, b % 2, :], ACT.Ln, bias=1.0)
+                nc.scalar.activation(lg, e[b // 2][:, b % 2, :], ACT.Ln, bias=one[:])
             nc.vector.scalar_tensor_tensor(res[:], lg, LOG_CAP, u[:, b, :], ALU.min, ALU.max)
             nc.sync.dma_start(out[b * P : (b + 1) * P, :], res[:])

from contextlib import ExitStack

import concourse.mybir as mybir
from concourse.masks import make_identity

F32 = mybir.dt.float32
BF16 = mybir.dt.bfloat16
I32 = mybir.dt.int32
U32 = mybir.dt.uint32
U16 = mybir.dt.uint16
U8 = mybir.dt.uint8
FP8X4 = mybir.dt.float8_e4m3fn_x4
ALU = mybir.AluOpType
ACT = mybir.ActivationFunctionType
AXIS = mybir.AxisListType

P = 128
PACK = 4
K, T, S, H, D, W, U = 512, 1024, 512, 512, 4, 2048, 512
V = U // D
BLOCKS = S // P
MARGIN = 0.3
E_CUT = 512
ROW0 = P - 16
LOG_CAP = 44.0

FLOPS = 2 * K * H * S + 2 * 2 * H * S * U


def tile_picked_yhard_soft_p_kernel(
    tc, x_words, x_scales, w1, e_words, e_scales, offs, pos, neg, out
):
    nc = tc.nc
    with ExitStack() as ctx:
        keep = ctx.enter_context(tc.tile_pool(name="keep", bufs=1))
        shared = ctx.enter_context(tc.tile_pool(name="shared", bufs=1))
        late = ctx.enter_context(tc.tile_pool(name="late", bufs=1))
        tail = ctx.enter_context(tc.tile_pool(name="tail", bufs=1))
        psum = ctx.enter_context(tc.psum_pool(name="psum", bufs=4))

        offs_t = keep.tile([P, S // 16], U16, name="offs_t")
        neg_t = keep.tile([P, U // 16], U16, name="neg_t")
        pos_t = keep.tile([P, U // 16], U16, name="pos_t")
        xs = shared.tile([P, T], U8, name="xs", offset=4 * E_CUT, align_bytes=64)
        es = keep.tile([P, W], U8, name="es", align_bytes=64)
        xw = keep.tile([P, T], I32, name="xw", align_bytes=64)
        w_raw = [keep.tile([P, PACK, H // 2], F32, name=f"w_raw{h}", tag=f"w_raw{h}", align_bytes=64) for h in range(2)]

        e_planes = keep.tile([P, 2 * U], U8, name="e_planes", align_bytes=64)
        x_plane = keep.tile([P, S], U8, name="x_plane", align_bytes=64)
        nc.vector.memset(xs[:ROW0, :].bitcast(I32), 0)
        nc.vector.memset(es[:ROW0, :].bitcast(I32), 0)
        zero = keep.tile([P, 1], F32, name="zero")
        one = keep.tile([P, 1], F32, name="one")
        nc.vector.memset(zero[:], 0.0)
        nc.vector.tensor_scalar(one[:], zero[:], 1.0, None, ALU.add)
        nc.vector.memset(x_plane[:].bitcast(I32), 0)
        nc.vector.memset(e_planes[:].bitcast(I32), 0)

        ident = keep.tile([P, P], F32, name="ident")
        make_identity(nc, ident[:])

        def place_rows(queues, plane, gathered):
            for q in range(4):
                queues[q % len(queues)].dma_start(plane[32 * q : 32 * q + 4, :].bitcast(I32), gathered[ROW0 + 4 * q : ROW0 + 4 * q + 4, :].bitcast(I32))

        w_rows = w1.rearrange("(p j) c -> p j c", j=PACK)
        nc.scalar.dma_start(xs[ROW0:, :].bitcast(I32), x_scales[0].bitcast(I32))
        nc.sync.dma_start(offs_t[:], offs)
        nc.sync.dma_start(neg_t[:], neg)
        nc.sync.dma_start(w_raw[0][:], w_rows[:, :, : H // 2])
        nc.scalar.dma_start(es[ROW0:, :].bitcast(I32), e_scales[0].bitcast(I32))
        nc.sync.dma_start(pos_t[:], pos)
        nc.sync.dma_start(w_raw[1][:], w_rows[:, :, H // 2 :])
        nc.sync.dma_start(xw[:], x_words[0].rearrange("p n t -> p (n t)").bitcast(I32))

        ew = shared.tile([P, W], I32, name="ew", offset=0, align_bytes=64)
        e_rows = e_words[0].rearrange("p n t -> p (n t)").bitcast(I32)
        nc.sync.dma_start(ew[:, :E_CUT], e_rows[:, :E_CUT])

        xs_g = keep.tile([P, S], U8, name="xs_g", align_bytes=64)
        es_g = late.tile([P, 2 * U], U8, name="es_g", offset=4 * S - U, align_bytes=64)
        nw_g = keep.tile([P, U], U32, name="nw_g", align_bytes=64)

        nc.vector.tensor_copy(xs_g[:], xs[:].indirect(offs_t[:]))
        place_rows((nc.sync,), x_plane, xs_g)
        nc.sync.dma_start(ew[:, E_CUT:], e_rows[:, E_CUT:])
        nc.vector.tensor_copy(es_g[:, :U], es[:].indirect(neg_t[:]))
        nc.vector.tensor_copy(es_g[:, U:], es[:].indirect(pos_t[:]))
        place_rows((nc.sync,), e_planes, es_g)

        xw_first = keep.tile([P, S // 2], U32, name="xw_first", align_bytes=64)
        nc.vector.tensor_copy(xw_first[:], xw[:].bitcast(U32).indirect(offs_t[:, : S // 32]))
        w_bf = keep.tile([P, PACK * H], BF16, name="w_bf", align_bytes=64)
        w_view = w_bf[:].rearrange("p (t m j) -> p m j t", t=PACK, j=PACK)
        for h in range(2):
            nc.scalar.activation(
                w_view[:, h * (P // 2) : (h + 1) * (P // 2), :, :],
                w_raw[h][:].rearrange("p j (m t) -> p m j t", t=PACK), ACT.Copy,
            )
        w_q = keep.tile([P, H], U32, name="w_q", align_bytes=64)
        w_s = keep.tile([P, H], U8, name="w_s", align_bytes=64)
        for half in range(2):
            words = slice(half * H // 2, (half + 1) * H // 2)
            values = slice(half * PACK * H // 2, (half + 1) * PACK * H // 2)
            nc.vector.quantize_mx(out=w_q[:, words].bitcast(FP8X4), scales=w_s[:, words], in_=w_bf[:, values])

        xw_g = keep.tile([P, S // 2], U32, name="xw_g", tag="w_raw1", align_bytes=64)
        x_codes = [(xw_first, xw_g)[b // 2][:, (b % 2) * P : (b % 2 + 1) * P] for b in range(BLOCKS)]
        nc.vector.tensor_copy(xw_g[:], xw[:].bitcast(U32).indirect(offs_t[:, S // 32 :]))

        h_q, h_s = [], []
        h_bf = []
        for b in range(BLOCKS):
            cols = slice(b * P, (b + 1) * P)
            bank = psum.tile([P, PACK, P], F32, name="hy", tag="hy")
            for t in range(PACK):
                wc = slice(t * P, (t + 1) * P)
                nc.tensor.matmul_mx(
                    out=bank[:, t, :], lhsT=w_q[:, wc].bitcast(FP8X4), lhsT_scale=w_s[:, wc],
                    rhs=x_codes[b].bitcast(FP8X4), rhs_scale=x_plane[:, cols], start=True, stop=True,
                )
            hb = keep.tile([P, P * PACK], BF16, name=f"h_bf{b}", align_bytes=64)
            nc.scalar.copy(hb[:].rearrange("p (n t) -> p n t", t=PACK), bank[:].rearrange("p t n -> p n t"))
            h_bf.append(hb)

        h_codes = late.tile([P, S], U32, name="h_codes", offset=0, align_bytes=64)
        pw_g = late.tile([P, U], U32, name="pw_g", offset=4 * S, align_bytes=64)
        nc.vector.tensor_copy(nw_g[:], ew[:].bitcast(U32).indirect(neg_t[:]))
        for b in range(BLOCKS):
            if b == 3:
                nc.vector.tensor_copy(pw_g[:], ew[:].bitcast(U32).indirect(pos_t[:]))
            hq = h_codes[:, b * P : (b + 1) * P]
            hs = keep.tile([P, P], U8, name=f"h_s{b}", align_bytes=64)
            nc.vector.quantize_mx(out=hq.bitcast(FP8X4), scales=hs[:], in_=h_bf[b][:])
            h_q.append(hq)
            h_s.append(hs)

        last = BLOCKS - 1
        z_pairs = keep.tile([P, BLOCKS, 2, V], F32, name="z_pairs")
        z_top = keep.tile([P, BLOCKS, V], F32, name="z_top")
        y_pairs = keep.tile([P, last, 2, V], F32, name="y_pairs")
        y_last_pairs = [tail.tile([P, V], F32, name="y_last0", offset=0), keep.tile([P, V], F32, name="y_last1")]
        u_pairs = keep.tile([P, 2, V], F32, name="u_pairs")
        e_pairs = keep.tile([P, BLOCKS, 2, V], F32, name="e_pairs")

        def product(b, tag, words, planes):
            bank = psum.tile([P, U], F32, name=tag, tag=tag)
            nc.tensor.matmul_mx(
                out=bank[:], lhsT=h_q[b].bitcast(FP8X4), lhsT_scale=h_s[b][:],
                rhs=words[:].bitcast(FP8X4), rhs_scale=planes, start=True, stop=True,
            )
            return bank[:].rearrange("p (v d) -> p d v", d=D)

        def negatives(b):
            z_d = product(b, "z", nw_g, e_planes[:, :U])
            z_lo = keep.tile([P, 2, V], F32, name=f"z_lo{b}")
            nc.scalar.activation(z_lo[:], z_d[:, 0:2, :], ACT.Copy, bias=MARGIN)
            nc.vector.scalar_tensor_tensor(z_pairs[:, b], z_d[:, 2:4, :], MARGIN, z_lo[:], ALU.add, ALU.max)

        def positives(b):
            y_d = product(b, "hy", pw_g, e_planes[:, U:])
            y_lo = keep.tile([P, 2, V], F32, name=f"y_lo{b}", tag=f"y_lo{b}")
            nc.scalar.activation(y_lo[:], y_d[:, 0:2, :], ACT.Copy, scale=-1.0)
            return y_d, y_lo

        def pair_up(b, y_d, y_lo):
            nc.vector.scalar_tensor_tensor(y_pairs[:, b], y_d[:, 2:4, :], -1.0, y_lo[:], ALU.mult, ALU.max)

        def pair_up_last(i, y_d, y_lo):
            nc.vector.scalar_tensor_tensor(y_last_pairs[i][:], y_d[:, 2 + i, :], -1.0, y_lo[:, i, :], ALU.mult, ALU.max)

        def fold(first, end):
            nc.vector.tensor_tensor(z_top[:, first:end, :], z_pairs[:, first:end, 0, :], z_pairs[:, first:end, 1, :], ALU.max)

        def margin(b):
            bank = psum.tile([V, PACK, P], F32, name="z", tag="z")
            for i in range(2):
                nc.tensor.matmul(bank[:, i, :], z_top[:, b, :], ident[:], start=True, stop=False, is_transpose=True)
                nc.tensor.matmul(bank[:, i, :], y_pairs[:, b, i, :], ident[:], start=False, stop=True, is_transpose=True)
            nc.scalar.activation(e_pairs[:, b], bank[:, 0:2, :], ACT.Exp)

        negatives(0)
        negatives(1)
        negatives(2)
        fold(0, 2)
        pair_up(0, *positives(0))
        fold(2, 3)
        pair_up(1, *positives(1))
        pair_up(2, *positives(2))
        negatives(3)
        y_last = positives(last)
        pair_up_last(0, *y_last)
        fold(last, BLOCKS)
        pair_up_last(1, *y_last)
        for b in range(last):
            margin(b)
        for i in range(2):
            nc.vector.tensor_tensor(u_pairs[:, i, :], y_last_pairs[i][:], z_top[:, last, :], ALU.add)
            nc.scalar.activation(e_pairs[:, last, i, :], u_pairs[:, i, :], ACT.Exp)

        u = keep.tile([P, BLOCKS, V], F32, name="u")
        y_top = tail.tile([P, last, V], F32, name="y_top", offset=0)
        e = [keep.tile([V, 2, P], F32, name=f"e{a}", tag=f"y_lo{last - a}") for a in range(2)]
        nc.vector.tensor_tensor(e[0][:], e_pairs[:, 0:2, 0, :], e_pairs[:, 0:2, 1, :], ALU.max)
        nc.vector.tensor_tensor(y_top[:], y_pairs[:, :, 0, :], y_pairs[:, :, 1, :], ALU.max)
        nc.vector.tensor_tensor(e[1][:], e_pairs[:, 2:4, 0, :], e_pairs[:, 2:4, 1, :], ALU.max)
        nc.vector.tensor_tensor(u[:, last, :], u_pairs[:, 0, :], u_pairs[:, 1, :], ALU.max)
        nc.vector.tensor_tensor(u[:, :last, :], z_top[:, :last, :], y_top[:], ALU.add)
        logs = tail.tile([P, BLOCKS, V], F32, name="logs", offset=0)
        for b in (last, 0, 1, 2):
            lg = logs[:, b, :]
            res = keep.tile([P, V], F32, name=f"res{b}")
            if b < last:
                back = psum.tile([P, PACK, V], F32, name="hy", tag="hy")
                nc.tensor.transpose(back[:, 0, :], e[b // 2][:, b % 2, :], ident[:])
                nc.scalar.activation(lg, back[:, 0, :], ACT.Ln, bias=one[:])
            else:
                nc.scalar.activation(lg, e[b // 2][:, b % 2, :], ACT.Ln, bias=one[:])
            nc.vector.scalar_tensor_tensor(res[:], lg, LOG_CAP, u[:, b, :], ALU.min, ALU.max)
            nc.sync.dma_start(out[b * P : (b + 1) * P, :], res[:])
